import numpy as np
import ml_dtypes

BF16 = ml_dtypes.bfloat16


def bf(x):
    return np.asarray(x, np.float32).astype(BF16)


def f32(x):
    return np.asarray(x, np.float32)


def f64(x):
    return np.asarray(x).astype(np.float64)


def striped(idx):
    return np.tile(idx.reshape(-1, 16).T, (8, 1))


A, S, K, M, N, E, Q = 256, 512, 256, 512, 128, 1, 128


def setup_inputs():
    return {"a": bf(np.random.standard_normal((A, S))), "wd": bf(np.random.standard_normal((A, M)) / np.sqrt(A)), "x": bf(np.random.standard_normal((K, N))), "w": bf(1.2 * np.random.standard_normal((E, K, M)) / np.sqrt(K)), "s": f32(0.5 + np.random.random_sample((M, 1))), "offs": striped(np.random.permutation(S)[:N])}


def reference(a, wd, x, w, s, offs):
    idx = offs[:16].T.reshape(-1)
    z = f64(wd).T @ f64(a)
    for e in range(E):
        z[:, idx[e * Q : (e + 1) * Q]] += f64(w)[e].T @ f64(x)[:, e * Q : (e + 1) * Q]
    z = z / np.sqrt((z**2).mean(axis=0, keepdims=True) + 1e-5) * f64(s)
    return z

@@ -1,0 +1,69 @@
+import concourse.mybir as mybir
+
+F32, BF16, U16 = mybir.dt.float32, mybir.dt.bfloat16, mybir.dt.uint16
+ACT = mybir.ActivationFunctionType
+MULT = mybir.AluOpType.mult
+
+P = 128
+D, M, TOKENS, N = 256, 512, 512, 128
+KB = D // P
+MB = M // P
+EPS = 1e-5
+
+FLOPS = 2 * D * M * (TOKENS + N)
+
+
+def tile_rows_placenorm_proj_kernel(tc, a, wd, x, w, s, offs, out):
+    nc = tc.nc
+    with (
+        tc.tile_pool(name="held", bufs=1) as held,
+        tc.psum_pool(name="psum", bufs=1) as psum,
+    ):
+        a_sb = held.tile([P, KB, TOKENS], BF16)
+        wd_sb = held.tile([P, KB, M], BF16)
+        x_sb = held.tile([P, KB, N], BF16)
+        w_sb = held.tile([P, KB, M], BF16)
+        offsets = held.tile([P, N // 16], U16)
+        gain = held.tile([P, MB], F32)
+        nc.sync.dma_start(a_sb[:], a.rearrange("(p k) i -> p k i", k=KB))
+        nc.sync.dma_start(wd_sb[:], wd.rearrange("(p k) m -> p k m", k=KB))
+        nc.sync.dma_start(offsets[:], offs)
+        nc.sync.dma_start(x_sb[:], x.rearrange("(p k) j -> p k j", k=KB))
+        nc.sync.dma_start(w_sb[:], w.rearrange("e (p k) m -> p (e k) m", k=KB))
+        nc.scalar.dma_start(gain[:], s.rearrange("(b p) o -> p (b o)", p=P))
+
+        averager = held.tile([P, P], BF16)
+        nc.vector.memset(averager[:], 1.0 / M)
+        eps = held.tile([P, 1], F32)
+        nc.vector.memset(eps[:], EPS)
+
+        windows = [psum.tile([P, TOKENS], F32, name=f"window{b}") for b in range(MB)]
+        for b in range(MB):
+            for k in range(KB):
+                nc.tensor.matmul(
+                    windows[b][:], wd_sb[:, k, b * P : (b + 1) * P], a_sb[:, k, :], start=k == 0, stop=False
+                )
+
+        for b in range(MB):
+            for k in range(KB):
+                nc.tensor.matmul(
+                    windows[b][:].indirect(offsets[:]),
+                    w_sb[:, k, b * P : (b + 1) * P],
+                    x_sb[:, k, :],
+                    start=False,
+                    stop=k == KB - 1,
+                )
+
+        mean = psum.tile([P, TOKENS], F32)
+        for b in range(MB):
+            squares = held.tile([P, TOKENS], BF16, name=f"squares{b}")
+            nc.scalar.activation(squares[:], windows[b][:], ACT.Square)
+            nc.tensor.matmul(mean[:], averager[:], squares[:], start=b == 0, stop=b == MB - 1)
+
+        rstd = held.tile([P, TOKENS], F32)
+        nc.scalar.activation(rstd[:], mean[:], ACT.Abs_reciprocal_sqrt, bias=eps[:])
+
+        for b in range(MB):
+            normed = held.tile([P, TOKENS], F32, name=f"normed{b}")
+            nc.vector.scalar_tensor_tensor(normed[:], windows[b][:], gain[:, b : b + 1], rstd[:], MULT, MULT)
+            nc.sync.dma_start(out[b * P : (b + 1) * P, :], normed[:])

@@ -7,8 +7,10 @@ MULT = mybir.AluOpType.mult
 P = 128
 D, M, TOKENS, N = 256, 512, 512, 128
 KB = D // P
+HALF = TOKENS // 2
 MB = M // P
 EPS = 1e-5
+WARM_UPS = 5
 
 FLOPS = 2 * D * M * (TOKENS + N)
 
@@ -37,6 +39,15 @@ def tile_rows_placenorm_proj_kernel(tc, a, wd, x, w, s, offs, out):
         eps = held.tile([P, 1], F32)
         nc.vector.memset(eps[:], EPS)
 
+        table_load = held.tile([P, 1], F32)
+        nc.scalar.activation(table_load[:], eps[:], ACT.Abs_reciprocal_sqrt)
+
+        zeros = held.tile([P, TOKENS], BF16)
+        nc.vector.memset(zeros[:], 0.0)
+        spare = psum.tile([P, TOKENS], F32)
+        for rep in range(WARM_UPS):
+            nc.tensor.matmul(spare[:], zeros[:, :P], zeros[:], start=True, stop=True)
+
         windows = [psum.tile([P, TOKENS], F32, name=f"window{b}") for b in range(MB)]
         for b in range(MB):
             for k in range(KB):
@@ -54,16 +65,26 @@ def tile_rows_placenorm_proj_kernel(tc, a, wd, x, w, s, offs, out):
                     stop=k == KB - 1,
                 )
 
-        mean = psum.tile([P, TOKENS], F32)
-        for b in range(MB):
-            squares = held.tile([P, TOKENS], BF16, name=f"squares{b}")
-            nc.scalar.activation(squares[:], windows[b][:], ACT.Square)
-            nc.tensor.matmul(mean[:], averager[:], squares[:], start=b == 0, stop=b == MB - 1)
+        means = [psum.tile([P, TOKENS], F32, name=f"mean{h}") for h in range(2)]
+        for h in range(2):
+            cols = slice(h * HALF, (h + 1) * HALF)
+            for b in range(MB):
+                squares = held.tile([P, HALF], BF16, name=f"squares{b}_{h}")
+                if b < MB - 1:
+                    nc.scalar.activation(squares[:], windows[b][:, cols], ACT.Square)
+                else:
+                    rounded = held.tile([P, HALF], BF16, name=f"rounded{h}")
+                    nc.vector.tensor_copy(rounded[:], windows[b][:, cols])
+                    nc.vector.tensor_tensor(squares[:], rounded[:], rounded[:], MULT)
+                nc.tensor.matmul(means[h][:, :HALF], averager[:], squares[:], start=b == 0, stop=b == MB - 1)
 
-        rstd = held.tile([P, TOKENS], F32)
-        nc.scalar.activation(rstd[:], mean[:], ACT.Abs_reciprocal_sqrt, bias=eps[:])
-
-        for b in range(MB):
-            normed = held.tile([P, TOKENS], F32, name=f"normed{b}")
-            nc.vector.scalar_tensor_tensor(normed[:], windows[b][:], gain[:, b : b + 1], rstd[:], MULT, MULT)
-            nc.sync.dma_start(out[b * P : (b + 1) * P, :], normed[:])
+        for h in range(2):
+            cols = slice(h * HALF, (h + 1) * HALF)
+            rstd = held.tile([P, HALF], F32, name=f"rstd{h}")
+            nc.scalar.activation(rstd[:], means[h][:, :HALF], ACT.Abs_reciprocal_sqrt, bias=eps[:])
+            for b in range(MB):
+                normed = held.tile([P, HALF], F32, name=f"normed{b}_{h}")
+                nc.vector.scalar_tensor_tensor(
+                    normed[:], windows[b][:, cols], gain[:, b : b + 1], rstd[:], MULT, MULT
+                )
+                nc.sync.dma_start(out[b * P : (b + 1) * P, cols], normed[:])

@@ -10,7 +10,7 @@ KB = D // P
 HALF = TOKENS // 2
 MB = M // P
 EPS = 1e-5
-WARM_UPS = 5
+WARM_UPS = 4
 
 FLOPS = 2 * D * M * (TOKENS + N)
 
@@ -21,18 +21,25 @@ def tile_rows_placenorm_proj_kernel(tc, a, wd, x, w, s, offs, out):
         tc.tile_pool(name="held", bufs=1) as held,
         tc.psum_pool(name="psum", bufs=1) as psum,
     ):
-        a_sb = held.tile([P, KB, TOKENS], BF16)
-        wd_sb = held.tile([P, KB, M], BF16)
+        a_sb = [held.tile([P, TOKENS], BF16, name=f"a{k}") for k in range(KB)]
+        wd_sb = [held.tile([P, M], BF16, name=f"wd{k}") for k in range(KB)]
         x_sb = held.tile([P, KB, N], BF16)
         w_sb = held.tile([P, KB, M], BF16)
         offsets = held.tile([P, N // 16], U16)
         gain = held.tile([P, MB], F32)
-        nc.sync.dma_start(a_sb[:], a.rearrange("(p k) i -> p k i", k=KB))
-        nc.sync.dma_start(wd_sb[:], wd.rearrange("(p k) m -> p k m", k=KB))
+        for k in range(KB):
+            nc.sync.dma_start(a_sb[k][:], a[k * P : (k + 1) * P, :])
+            nc.scalar.dma_start(wd_sb[k][:], wd[k * P : (k + 1) * P, :])
         nc.sync.dma_start(offsets[:], offs)
         nc.sync.dma_start(x_sb[:], x.rearrange("(p k) j -> p k j", k=KB))
-        nc.sync.dma_start(w_sb[:], w.rearrange("e (p k) m -> p (e k) m", k=KB))
+        nc.scalar.dma_start(w_sb[:], w.rearrange("e (p k) m -> p (e k) m", k=KB))
         nc.scalar.dma_start(gain[:], s.rearrange("(b p) o -> p (b o)", p=P))
+
+        zeros = held.tile([P, TOKENS], BF16)
+        nc.vector.memset(zeros[:], 0.0)
+        spare = psum.tile([P, TOKENS], F32)
+        for rep in range(WARM_UPS):
+            nc.tensor.matmul(spare[:], zeros[:, :P], zeros[:], start=True, stop=True)
 
         averager = held.tile([P, P], BF16)
         nc.vector.memset(averager[:], 1.0 / M)
@@ -42,17 +49,11 @@ def tile_rows_placenorm_proj_kernel(tc, a, wd, x, w, s, offs, out):
         table_load = held.tile([P, 1], F32)
         nc.scalar.activation(table_load[:], eps[:], ACT.Abs_reciprocal_sqrt)
 
-        zeros = held.tile([P, TOKENS], BF16)
-        nc.vector.memset(zeros[:], 0.0)
-        spare = psum.tile([P, TOKENS], F32)
-        for rep in range(WARM_UPS):
-            nc.tensor.matmul(spare[:], zeros[:, :P], zeros[:], start=True, stop=True)
-
         windows = [psum.tile([P, TOKENS], F32, name=f"window{b}") for b in range(MB)]
-        for b in range(MB):
-            for k in range(KB):
+        for k in range(KB):
+            for b in range(MB):
                 nc.tensor.matmul(
-                    windows[b][:], wd_sb[:, k, b * P : (b + 1) * P], a_sb[:, k, :], start=k == 0, stop=False
+                    windows[b][:], wd_sb[k][:, b * P : (b + 1) * P], a_sb[k][:], start=k == 0, stop=False
                 )
 
         for b in range(MB):
@@ -70,12 +71,12 @@ def tile_rows_placenorm_proj_kernel(tc, a, wd, x, w, s, offs, out):
             cols = slice(h * HALF, (h + 1) * HALF)
             for b in range(MB):
                 squares = held.tile([P, HALF], BF16, name=f"squares{b}_{h}")
-                if b < MB - 1:
-                    nc.scalar.activation(squares[:], windows[b][:, cols], ACT.Square)
-                else:
-                    rounded = held.tile([P, HALF], BF16, name=f"rounded{h}")
+                if b < MB // 2:
+                    rounded = held.tile([P, HALF], BF16, name=f"rounded{b}_{h}")
                     nc.vector.tensor_copy(rounded[:], windows[b][:, cols])
                     nc.vector.tensor_tensor(squares[:], rounded[:], rounded[:], MULT)
+                else:
+                    nc.scalar.activation(squares[:], windows[b][:, cols], ACT.Square)
                 nc.tensor.matmul(means[h][:, :HALF], averager[:], squares[:], start=b == 0, stop=b == MB - 1)
 
         for h in range(2):

import concourse.mybir as mybir

F32, BF16, U16 = mybir.dt.float32, mybir.dt.bfloat16, mybir.dt.uint16
ACT = mybir.ActivationFunctionType
MULT = mybir.AluOpType.mult

P = 128
D, M, TOKENS, N = 256, 512, 512, 128
KB = D // P
HALF = TOKENS // 2
MB = M // P
EPS = 1e-5
WARM_UPS = 4

FLOPS = 2 * D * M * (TOKENS + N)


def tile_rows_placenorm_proj_kernel(tc, a, wd, x, w, s, offs, out):
    nc = tc.nc
    with (
        tc.tile_pool(name="held", bufs=1) as held,
        tc.psum_pool(name="psum", bufs=1) as psum,
    ):
        a_sb = [held.tile([P, TOKENS], BF16, name=f"a{k}") for k in range(KB)]
        wd_sb = [held.tile([P, M], BF16, name=f"wd{k}") for k in range(KB)]
        x_sb = held.tile([P, KB, N], BF16)
        w_sb = held.tile([P, KB, M], BF16)
        offsets = held.tile([P, N // 16], U16)
        gain = held.tile([P, MB], F32)
        for k in range(KB):
            nc.sync.dma_start(a_sb[k][:], a[k * P : (k + 1) * P, :])
            nc.scalar.dma_start(wd_sb[k][:], wd[k * P : (k + 1) * P, :])
        nc.sync.dma_start(offsets[:], offs)
        nc.sync.dma_start(x_sb[:], x.rearrange("(p k) j -> p k j", k=KB))
        nc.scalar.dma_start(w_sb[:], w.rearrange("e (p k) m -> p (e k) m", k=KB))
        nc.scalar.dma_start(gain[:], s.rearrange("(b p) o -> p (b o)", p=P))

        zeros = held.tile([P, TOKENS], BF16)
        nc.vector.memset(zeros[:], 0.0)
        spare = psum.tile([P, TOKENS], F32)
        for rep in range(WARM_UPS):
            nc.tensor.matmul(spare[:], zeros[:, :P], zeros[:], start=True, stop=True)

        averager = held.tile([P, P], BF16)
        nc.vector.memset(averager[:], 1.0 / M)
        eps = held.tile([P, 1], F32)
        nc.vector.memset(eps[:], EPS)

        table_load = held.tile([P, 1], F32)
        nc.scalar.activation(table_load[:], eps[:], ACT.Abs_reciprocal_sqrt)

        windows = [psum.tile([P, TOKENS], F32, name=f"window{b}") for b in range(MB)]
        for k in range(KB):
            for b in range(MB):
                nc.tensor.matmul(
                    windows[b][:], wd_sb[k][:, b * P : (b + 1) * P], a_sb[k][:], start=k == 0, stop=False
                )

        for b in range(MB):
            for k in range(KB):
                nc.tensor.matmul(
                    windows[b][:].indirect(offsets[:]),
                    w_sb[:, k, b * P : (b + 1) * P],
                    x_sb[:, k, :],
                    start=False,
                    stop=k == KB - 1,
                )

        means = [psum.tile([P, TOKENS], F32, name=f"mean{h}") for h in range(2)]
        for h in range(2):
            cols = slice(h * HALF, (h + 1) * HALF)
            for b in range(MB):
                squares = held.tile([P, HALF], BF16, name=f"squares{b}_{h}")
                if b < MB // 2:
                    rounded = held.tile([P, HALF], BF16, name=f"rounded{b}_{h}")
                    nc.vector.tensor_copy(rounded[:], windows[b][:, cols])
                    nc.vector.tensor_tensor(squares[:], rounded[:], rounded[:], MULT)
                else:
                    nc.scalar.activation(squares[:], windows[b][:, cols], ACT.Square)
                nc.tensor.matmul(means[h][:, :HALF], averager[:], squares[:], start=b == 0, stop=b == MB - 1)

        for h in range(2):
            cols = slice(h * HALF, (h + 1) * HALF)
            rstd = held.tile([P, HALF], F32, name=f"rstd{h}")
            nc.scalar.activation(rstd[:], means[h][:, :HALF], ACT.Abs_reciprocal_sqrt, bias=eps[:])
            for b in range(MB):
                normed = held.tile([P, HALF], F32, name=f"normed{b}_{h}")
                nc.vector.scalar_tensor_tensor(
                    normed[:], windows[b][:, cols], gain[:, b : b + 1], rstd[:], MULT, MULT
                )
                nc.sync.dma_start(out[b * P : (b + 1) * P, cols], normed[:])
